import numpy as np
import ml_dtypes


def mxq(x, axis, fmt="e4m3"):
    dtype, down = {"e4m3": (ml_dtypes.float8_e4m3fn, 7), "e5m2": (ml_dtypes.float8_e5m2, 14)}[fmt]
    v = np.moveaxis(np.asarray(x, np.float32).astype(ml_dtypes.bfloat16).astype(np.float64), axis, -1)
    blocks = v.reshape(v.shape[:-1] + (-1, 32))
    amax = np.abs(blocks).max(-1, keepdims=True)
    byte = np.maximum(np.where(amax > 0, np.frexp(amax)[1] - 1 + 127, 0) - down, 1)
    scale = np.exp2(byte - 127.0)
    codes = (blocks / scale).astype(np.float32).astype(dtype).astype(np.float64)
    return np.moveaxis((codes * scale).reshape(v.shape), -1, axis)


WIDE = False


def mx_kscale(k):
    if not WIDE:
        return np.ones(k)
    levels = np.array([10, -10, 5, -5, 0])
    if k % 512:
        return np.exp2(np.random.permutation(np.resize(levels, k // 32))).repeat(32)
    a = np.empty((k // 512, 16))
    for p in range(k // 512):
        a[p, :8] = np.random.permutation(np.resize(levels, 8))
        for g in range(8):
            far = levels[np.abs(levels - a[p, g]) >= 10]
            a[p, g + 8] = far[np.random.randint(len(far))]
    return np.exp2(a.ravel()).repeat(32)


def f64(x):
    return np.asarray(x).astype(np.float64)


def striped(idx):
    return np.tile(idx.reshape(-1, 16).T, (8, 1)).astype(np.uint16)


def unstriped(offs):
    return offs[:16].T.reshape(-1).astype(np.int64)


def striped8(idx):
    return np.concatenate([x.reshape(-1, 16).T for x in idx]).astype(np.uint16)


def runs(offs, k):
    lists = np.stack([offs[16 * r : 16 * r + 16].T.reshape(-1) for r in range(8)]).astype(np.int64)
    return lists[np.arange(k) % 512 // 64]


def pack_weight(w):
    k, n = w.shape
    w = f64(np.asarray(w, np.float32).astype(ml_dtypes.bfloat16)).reshape(k // 32, 32, n)
    amax = np.abs(w).max(1)
    byte = np.clip(np.where(amax > 0, np.frexp(amax)[1] - 1 + 127 - 7, 1), 1, 254)
    scaled = (w * np.exp2(127.0 - byte)[:, None, :]).reshape(k, n).astype(np.float32)
    words = np.ascontiguousarray(scaled.reshape(k // 512, 128, 4, n).transpose(0, 1, 3, 2)).astype(ml_dtypes.float8_e4m3fn).view(np.uint8)
    return words, np.ascontiguousarray(byte.astype(np.uint8).reshape(k // 512, 16, n))


def unpack_weight(words, scales):
    g, p, n, _ = words.shape
    vals = np.ascontiguousarray(words).view(ml_dtypes.float8_e4m3fn).astype(np.float64) * np.repeat(np.exp2(scales.astype(np.float64) - 127.0), 8, axis=1)[..., None]
    return vals.transpose(0, 1, 3, 2).reshape(g * 512, n)


K, T, S, N, H = 512, 2048, 256, 512, 512


def setup_inputs():
    n = np.random.standard_normal
    s = mx_kscale(K)[:, None]
    u = mx_kscale(H)
    packed_xT = pack_weight(n((K, T)) * s)
    return {
        "x_words": packed_xT[0],
        "x_scales": packed_xT[1],
        "w1": (n((K, H)) / np.sqrt(K) / s).astype(np.float32),
        "gn": (np.random.uniform(0.5, 1.5, (H, 1)) * u[:, None]).astype(np.float32),
        "w2": (n((H, N)) / np.sqrt(2 * H) / u[:, None]).astype(np.float32),
        "w3": (n((K, N)) / np.sqrt(2 * K) / s).astype(np.float32),
        "tau": np.random.uniform(0.3, 0.9, (N, 1)).astype(np.float32),
        "offs": striped8(np.random.randint(0, T, (8, S))),
        "n1": striped(np.random.permutation(S)),
        "two": striped(np.random.permutation(T)[:S]),
        "n2": striped8(np.stack([np.random.permutation(S) for _ in range(8)])),
        "n3": striped8(np.stack([np.random.permutation(S) for _ in range(8)])),
    }


def reference(x_words, x_scales, w1, gn, w2, w3, tau, offs, n1, two, n2, n3):
    xq = unpack_weight(x_words, x_scales)[np.arange(K)[:, None], runs(offs, K)]
    y = mxq(f64(w1), 0, "e4m3").T @ xq
    pa = y[:, unstriped(n1)]
    z = f64(gn) * ((2.0 * (y * pa)) / ((y) ** 2 + (pa) ** 2 + 0.5))
    x_two = unpack_weight(x_words, x_scales)[:, unstriped(two)]
    h = mxq(f64(w2), 0, "e4m3").T @ mxq(z, 0, "e4m3") + mxq(f64(w3), 0, "e4m3").T @ x_two
    top = h.max(axis=1, keepdims=True)
    ea = np.exp(f64(tau) * (h[np.arange(N)[:, None], runs(n2, N)] - top))
    ea2 = np.exp(f64(tau) * (h[np.arange(N)[:, None], runs(n3, N)] - top))
    return h + np.log(ea + ea2 + 0.25)

@@ -1,0 +1,209 @@
+from contextlib import ExitStack
+
+import concourse.mybir as mybir
+
+K, T, S, N, H = 512, 2048, 256, 512, 512
+FLOPS = 2 * S * (K * H + H * N + K * N)
+
+F32 = mybir.dt.float32
+BF16 = mybir.dt.bfloat16
+I32 = mybir.dt.int32
+U32 = mybir.dt.uint32
+U16 = mybir.dt.uint16
+U8 = mybir.dt.uint8
+FP8X4 = mybir.dt.float8_e4m3fn_x4
+ACT = mybir.ActivationFunctionType
+ALU = mybir.AluOpType
+
+P = 128
+PACK = 4
+HALF = S // 2
+M_SPLIT = 104
+
+
+def tile_picked_hmixharmelg_none_p_kernel(tc, x_words, x_scales, w1, gn, w2, w3, tau, offs, n1, two, n2, n3, out):
+    nc = tc.nc
+    with ExitStack() as ctx:
+        keep = ctx.enter_context(tc.tile_pool(name="keep", bufs=1))
+        psum = ctx.enter_context(tc.psum_pool(name="psum", bufs=1))
+
+        def load_list(src, name):
+            tile = keep.tile([P, S // 16], U16, name=name)
+            nc.sync.dma_start(tile[:], src)
+            return tile
+
+        scale_table = keep.tile([P, T], U8, name="scale_table", align_bytes=64)
+        nc.vector.memset(scale_table[:].bitcast(I32), 0)
+        offs_sb = load_list(offs, "offs_sb")
+        two_sb = load_list(two, "two_sb")
+        scale_rows = x_scales[0].bitcast(I32)
+        for b in range(2):
+            nc.sync.dma_start(scale_table[:].bitcast(I32)[b:P:16, :], scale_rows[b:16:2, :])
+        word_table = keep.tile([P, T], I32, name="word_table", align_bytes=64)
+        nc.sync.dma_start(word_table[:], x_words[0].rearrange("p n t -> p (n t)").bitcast(I32))
+
+        w1_halves = keep.tile([P, 2, PACK, H // 2], F32, name="w1_halves", tag="w1_then_w2")
+        w1_raw = [w1_halves[:, half] for half in range(2)]
+        for half in range(2):
+            nc.sync.dma_start(w1_raw[half], w1.rearrange("(p j) c -> p j c", j=PACK)[:, :, 256 * half : 256 * (half + 1)])
+        w3_raw = keep.tile([P, PACK, N], F32, name="w3_raw")
+        nc.sync.dma_start(w3_raw[:], w3.rearrange("(p j) c -> p j c", j=PACK))
+        n1_sb = load_list(n1, "n1_sb")
+        n2_sb = load_list(n2, "n2_sb")
+        n3_sb = load_list(n3, "n3_sb")
+        gn_sb = keep.tile([P, PACK], F32, name="gn_sb")
+        nc.scalar.dma_start(gn_sb[:], gn.rearrange("(p t) o -> p (t o)", t=PACK))
+        tau_sb = keep.tile([P, PACK], F32, name="tau_sb")
+        nc.scalar.dma_start(tau_sb[:], tau.rearrange("(p t) o -> p (t o)", t=PACK))
+
+        h_win = [keep.tile([P, 2 * S], F32, name="h_win%d" % t) for t in range(PACK)]
+        for t in range(PACK):
+            nc.vector.memset(h_win[t][:, S:], 0.0)
+
+        picked_bytes = keep.tile([P, 2 * S], U8, name="picked_bytes", align_bytes=64)
+        nc.vector.tensor_copy(picked_bytes[:, :S], scale_table[:].indirect(offs_sb[:]))
+        nc.vector.tensor_copy(picked_bytes[:, S:], scale_table[:].indirect(two_sb[:]))
+        x_plane = keep.tile([P, 2 * S], U8, name="x_plane", align_bytes=64)
+        nc.vector.tensor_copy(x_plane[:].bitcast(I32), picked_bytes[:].bitcast(I32))
+        for b in range(2):
+            nc.scalar.dma_start(x_plane[:].bitcast(I32)[2 + b : P : 32, :], picked_bytes[:].bitcast(I32)[16 + b : P : 32, :])
+
+        xq_words = keep.tile([P, S], U32, name="xq_words", align_bytes=64)
+        nc.vector.tensor_copy(xq_words[:], word_table[:].bitcast(U32).indirect(offs_sb[:]))
+        xtwo_words = keep.tile([P, S], U32, name="xtwo_words", align_bytes=64)
+        nc.vector.tensor_copy(xtwo_words[:], word_table[:].bitcast(U32).indirect(two_sb[:]))
+
+        def deal(copy, dealt, raw, m_raw, m_lo, m_hi, t_lo=0, t_hi=PACK):
+            copy(
+                dealt[:, :, m_lo:m_hi, :].rearrange("p t m j -> p m j t"),
+                raw.rearrange("p j (m t) -> p m j t", t=PACK)[:, m_lo - m_raw : m_hi - m_raw, :, t_lo:t_hi],
+            )
+
+        def mx_tiles(name, width):
+            words = keep.tile([P, width], U32, name=name + "_words", align_bytes=64)
+            plane = keep.tile([P, width], U8, name=name + "_plane", align_bytes=64)
+            return words, plane
+
+        w1_bf = keep.tile([P, PACK, P, PACK], BF16, name="w1_bf", align_bytes=64)
+        deal(nc.vector.tensor_copy, w1_bf, w1_raw[0], 0, 0, 64)
+        deal(nc.vector.tensor_copy, w1_bf, w1_raw[1], 64, 64, M_SPLIT)
+        deal(nc.scalar.copy, w1_bf, w1_raw[1], 64, M_SPLIT, P)
+        w2_raw = keep.tile([P, PACK, N], F32, name="w2_raw", tag="w1_then_w2")
+        nc.sync.dma_start(w2_raw[:], w2.rearrange("(p j) c -> p j c", j=PACK))
+
+        y_ps = [psum.tile([P, S], F32, name="y_ps%d" % t) for t in range(PACK)]
+        y_win = [keep.tile([P, S], F32, name="y_win%d" % t) for t in range(PACK)]
+        for t in range(PACK):
+            words, plane = mx_tiles("w1_%d" % t, P)
+            nc.vector.quantize_mx(words[:].bitcast(FP8X4), plane[:], w1_bf[:, t].rearrange("p m j -> p (m j)"))
+            nc.tensor.matmul_mx(
+                y_ps[t][:], lhsT=words[:].bitcast(FP8X4), lhsT_scale=plane[:],
+                rhs=xq_words[:].bitcast(FP8X4), rhs_scale=x_plane[:, :S], start=True, stop=True,
+            )
+        for t in range(PACK):
+            nc.vector.tensor_copy(y_win[t][:], y_ps[t][:])
+
+        def halves(name):
+            return [keep.tile([P, PACK, HALF], F32, name="%s%d" % (name, half)) for half in range(2)]
+
+        pa, pa_sq, num, sq_sum, root, inv = (halves(name) for name in ("pa", "pa_sq", "num", "sq_sum", "root", "inv"))
+        y_sq = keep.tile([P, 2, PACK, HALF], F32, name="y_sq")
+        z_words, z_plane = mx_tiles("z", S)
+
+        def fetch(half):
+            for t in range(PACK):
+                nc.scalar.activation(pa[half][:, t, :], y_win[t][:].indirect(n1_sb[:, 8 * half : 8 * (half + 1)]), ACT.Copy)
+
+        def numerator(half):
+            for t in range(PACK):
+                nc.vector.scalar_tensor_tensor(
+                    num[half][:, t, :], pa[half][:, t, :], gn_sb[:, t : t + 1],
+                    y_ps[t][:, HALF * half : HALF * (half + 1)], ALU.mult, ALU.mult,
+                )
+
+        def square_sum(half):
+            nc.scalar.activation(pa_sq[half][:], pa[half][:], ACT.Square)
+            nc.vector.tensor_tensor(sq_sum[half][:], pa_sq[half][:], y_sq[:, half], ALU.add)
+
+        def inverse(half):
+            nc.scalar.activation(root[half][:], sq_sum[half][:], ACT.Abs_reciprocal_sqrt, bias=0.25, scale=0.5)
+            nc.scalar.activation(inv[half][:], root[half][:], ACT.Square)
+
+        def make_z(half):
+            z_bf = keep.tile([P, HALF, PACK], BF16, name="z_bf%d" % half, align_bytes=64)
+            nc.vector.tensor_tensor(
+                z_bf[:].rearrange("p (c i) t -> p c t i", i=4),
+                num[half][:].rearrange("p t (c i) -> p c t i", i=4),
+                inv[half][:].rearrange("p t (c i) -> p c t i", i=4),
+                ALU.mult,
+            )
+            cols = slice(HALF * half, HALF * (half + 1))
+            nc.vector.quantize_mx(z_words[:, cols].bitcast(FP8X4), z_plane[:, cols], z_bf[:].rearrange("p c t -> p (c t)"))
+
+        w3_bf = keep.tile([P, PACK, P, PACK], BF16, name="w3_bf", align_bytes=64)
+        w3_words, w3_plane = mx_tiles("w3", N)
+        w2_mx = [mx_tiles("w2_%d" % pair, N // 2) for pair in range(2)]
+        w2_bf = [keep.tile([P, 2, P, PACK], BF16, name="w2_bf%d" % pair, align_bytes=64) for pair in range(2)]
+
+        def round_w2(pair):
+            deal(nc.vector.tensor_copy, w2_bf[pair], w2_raw[:], 0, 0, P, 2 * pair, 2 * pair + 2)
+
+        def quantize_w2(pair):
+            words, plane = w2_mx[pair]
+            nc.vector.quantize_mx(words[:].bitcast(FP8X4), plane[:], w2_bf[pair][:].rearrange("p t m j -> p (t m j)"))
+
+        fetch(0)
+        for t in range(PACK):
+            nc.scalar.activation(y_sq[:, :, t, :], y_win[t][:].rearrange("p (u c) -> p u c", u=2), ACT.Square)
+        deal(nc.vector.tensor_copy, w3_bf, w3_raw[:], 0, 0, P)
+        numerator(0)
+        square_sum(0)
+        fetch(1)
+        nc.vector.quantize_mx(w3_words[:].bitcast(FP8X4), w3_plane[:], w3_bf[:].rearrange("p t m j -> p (t m j)"))
+        inverse(0)
+        round_w2(0)
+        square_sum(1)
+        numerator(1)
+        inverse(1)
+        quantize_w2(0)
+        make_z(0)
+        make_z(1)
+
+        h_ps = [psum.tile([P, S], F32, name="h_ps%d" % t) for t in range(PACK)]
+        for t in range(PACK):
+            cols = slice(P * t, P * (t + 1))
+            nc.tensor.matmul_mx(
+                h_ps[t][:], lhsT=w3_words[:, cols].bitcast(FP8X4), lhsT_scale=w3_plane[:, cols],
+                rhs=xtwo_words[:].bitcast(FP8X4), rhs_scale=x_plane[:, S:], start=True, stop=False,
+            )
+
+        top = keep.tile([P, PACK], F32, name="top")
+        shift = keep.tile([P, PACK], F32, name="shift", tag="shift_then_log")
+        ea = keep.tile([P, PACK, S], F32, name="ea")
+        ea2 = keep.tile([P, PACK, S], F32, name="ea2")
+        ea_sum = keep.tile([P, PACK, S], F32, name="ea_sum")
+        for t in range(PACK):
+            if t == 2:
+                round_w2(1)
+                quantize_w2(1)
+            words, plane = w2_mx[t // 2]
+            cols = slice(P * (t % 2), P * (t % 2 + 1))
+            nc.tensor.matmul_mx(
+                h_ps[t][:], lhsT=words[:, cols].bitcast(FP8X4), lhsT_scale=plane[:, cols],
+                rhs=z_words[:].bitcast(FP8X4), rhs_scale=z_plane[:], start=False, stop=True,
+            )
+            col = slice(t, t + 1)
+            nc.vector.tensor_scalar(h_win[t][:, :S], h_ps[t][:], 1.0, None, ALU.mult, ALU.max, accum_out=top[:, col])
+            nc.vector.tensor_scalar(shift[:, col], top[:, col], tau_sb[:, col], -1.0, ALU.mult, ALU.mult)
+            nc.scalar.activation(ea[:, t, :], h_win[t][:].indirect(n2_sb[:]), ACT.Exp, bias=shift[:, col], scale=tau_sb[:, col])
+            nc.scalar.activation(ea2[:, t, :], h_win[t][:].indirect(n3_sb[:]), ACT.Exp, bias=shift[:, col], scale=tau_sb[:, col])
+        for t in range(PACK):
+            nc.vector.tensor_tensor(ea_sum[:, t, :], ea[:, t, :], ea2[:, t, :], ALU.add)
+
+        logs = keep.tile([P, PACK, S], F32, name="logs", tag="shift_then_log")
+        res = keep.tile([P, PACK, S], F32, name="res")
+        out_rows = out.rearrange("(p t) j -> p t j", t=PACK)
+        for t in range(PACK):
+            nc.scalar.activation(logs[:, t, :], ea_sum[:, t, :], ACT.Ln, bias=0.25)
+            nc.vector.tensor_tensor(res[:, t, :], h_ps[t][:], logs[:, t, :], ALU.add)
+            nc.sync.dma_start(out_rows[:, t, :], res[:, t, :])

@@ -56,6 +56,11 @@ def tile_picked_hmixharmelg_none_p_kernel(tc, x_words, x_scales, w1, gn, w2, w3,
         tau_sb = keep.tile([P, PACK], F32, name="tau_sb")
         nc.scalar.dma_start(tau_sb[:], tau.rearrange("(p t) o -> p (t o)", t=PACK))
 
+        warm_in = keep.tile([P, 1], F32, name="warm_in")
+        warm_out = keep.tile([P, 1], F32, name="warm_out")
+        nc.gpsimd.memset(warm_in[:], 1.0)
+        nc.scalar.activation(warm_out[:], warm_in[:], ACT.Abs_reciprocal_sqrt, bias=0.25, scale=0.5)
+
         h_win = [keep.tile([P, 2 * S], F32, name="h_win%d" % t) for t in range(PACK)]
         for t in range(PACK):
             nc.vector.memset(h_win[t][:, S:], 0.0)

@@ -19,6 +19,7 @@ P = 128
 PACK = 4
 HALF = S // 2
 M_SPLIT = 104
+X_SPLIT = 512
 
 
 def tile_picked_hmixharmelg_none_p_kernel(tc, x_words, x_scales, w1, gn, w2, w3, tau, offs, n1, two, n2, n3, out):
@@ -32,29 +33,26 @@ def tile_picked_hmixharmelg_none_p_kernel(tc, x_words, x_scales, w1, gn, w2, w3,
             nc.sync.dma_start(tile[:], src)
             return tile
 
-        scale_table = keep.tile([P, T], U8, name="scale_table", align_bytes=64)
-        nc.vector.memset(scale_table[:].bitcast(I32), 0)
+        scale_table = keep.tile([P, T], U8, name="scale_table", tag="scales_then_w3", align_bytes=64)
+        nc.vector.memset(scale_table[:, : T // 2].bitcast(I32), 0)
+        nc.gpsimd.memset(scale_table[:, T // 2 :].bitcast(I32), 0)
+        word_table = keep.tile([P, T], I32, name="word_table", tag="words_then_gn", align_bytes=64)
+        word_rows = x_words[0].rearrange("p n t -> p (n t)").bitcast(I32)
+        nc.sync.dma_start(word_table[:, :X_SPLIT], word_rows[:, :X_SPLIT])
         offs_sb = load_list(offs, "offs_sb")
         two_sb = load_list(two, "two_sb")
+        n1_sb = load_list(n1, "n1_sb")
         scale_rows = x_scales[0].bitcast(I32)
         for b in range(2):
             nc.sync.dma_start(scale_table[:].bitcast(I32)[b:P:16, :], scale_rows[b:16:2, :])
-        word_table = keep.tile([P, T], I32, name="word_table", align_bytes=64)
-        nc.sync.dma_start(word_table[:], x_words[0].rearrange("p n t -> p (n t)").bitcast(I32))
+        nc.sync.dma_start(word_table[:, X_SPLIT:], word_rows[:, X_SPLIT:])
 
         w1_halves = keep.tile([P, 2, PACK, H // 2], F32, name="w1_halves", tag="w1_then_w2")
         w1_raw = [w1_halves[:, half] for half in range(2)]
         for half in range(2):
             nc.sync.dma_start(w1_raw[half], w1.rearrange("(p j) c -> p j c", j=PACK)[:, :, 256 * half : 256 * (half + 1)])
-        w3_raw = keep.tile([P, PACK, N], F32, name="w3_raw")
-        nc.sync.dma_start(w3_raw[:], w3.rearrange("(p j) c -> p j c", j=PACK))
-        n1_sb = load_list(n1, "n1_sb")
         n2_sb = load_list(n2, "n2_sb")
         n3_sb = load_list(n3, "n3_sb")
-        gn_sb = keep.tile([P, PACK], F32, name="gn_sb")
-        nc.scalar.dma_start(gn_sb[:], gn.rearrange("(p t) o -> p (t o)", t=PACK))
-        tau_sb = keep.tile([P, PACK], F32, name="tau_sb")
-        nc.scalar.dma_start(tau_sb[:], tau.rearrange("(p t) o -> p (t o)", t=PACK))
 
         warm_in = keep.tile([P, 1], F32, name="warm_in")
         warm_out = keep.tile([P, 1], F32, name="warm_out")
@@ -62,21 +60,32 @@ def tile_picked_hmixharmelg_none_p_kernel(tc, x_words, x_scales, w1, gn, w2, w3,
         nc.scalar.activation(warm_out[:], warm_in[:], ACT.Abs_reciprocal_sqrt, bias=0.25, scale=0.5)
 
         h_win = [keep.tile([P, 2 * S], F32, name="h_win%d" % t) for t in range(PACK)]
+        y_win = [keep.tile([P, S + 16], F32, name="y_win%d" % t) for t in range(PACK)]
         for t in range(PACK):
+            nc.vector.memset(y_win[t][:, S:], 0.0)
             nc.vector.memset(h_win[t][:, S:], 0.0)
 
-        picked_bytes = keep.tile([P, 2 * S], U8, name="picked_bytes", align_bytes=64)
+        x_plane = keep.tile([P, 2 * S], U8, name="x_plane", align_bytes=64)
+        nc.vector.memset(x_plane[:].bitcast(I32), 0)
+        picked_bytes = keep.tile([P, 2 * S], U8, name="picked_bytes", tag="bytes_then_tau", align_bytes=64)
         nc.vector.tensor_copy(picked_bytes[:, :S], scale_table[:].indirect(offs_sb[:]))
         nc.vector.tensor_copy(picked_bytes[:, S:], scale_table[:].indirect(two_sb[:]))
-        x_plane = keep.tile([P, 2 * S], U8, name="x_plane", align_bytes=64)
-        nc.vector.tensor_copy(x_plane[:].bitcast(I32), picked_bytes[:].bitcast(I32))
+        for q in range(4):
+            rows = slice(32 * q, 32 * q + 2)
+            nc.vector.tensor_copy(x_plane[:].bitcast(I32)[rows, :], picked_bytes[:].bitcast(I32)[rows, :])
         for b in range(2):
-            nc.scalar.dma_start(x_plane[:].bitcast(I32)[2 + b : P : 32, :], picked_bytes[:].bitcast(I32)[16 + b : P : 32, :])
+            nc.sync.dma_start(x_plane[:].bitcast(I32)[2 + b : P : 32, :], picked_bytes[:].bitcast(I32)[16 + b : P : 32, :])
+        w3_raw = keep.tile([P, PACK, N], F32, name="w3_raw", tag="scales_then_w3", align_bytes=64)
+        nc.sync.dma_start(w3_raw[:], w3.rearrange("(p j) c -> p j c", j=PACK))
 
         xq_words = keep.tile([P, S], U32, name="xq_words", align_bytes=64)
         nc.vector.tensor_copy(xq_words[:], word_table[:].bitcast(U32).indirect(offs_sb[:]))
         xtwo_words = keep.tile([P, S], U32, name="xtwo_words", align_bytes=64)
         nc.vector.tensor_copy(xtwo_words[:], word_table[:].bitcast(U32).indirect(two_sb[:]))
+        gn_sb = keep.tile([P, PACK], F32, name="gn_sb", tag="words_then_gn", align_bytes=64)
+        nc.sync.dma_start(gn_sb[:], gn.rearrange("(p t) o -> p (t o)", t=PACK))
+        tau_sb = keep.tile([P, PACK], F32, name="tau_sb", tag="bytes_then_tau", align_bytes=64)
+        nc.sync.dma_start(tau_sb[:], tau.rearrange("(p t) o -> p (t o)", t=PACK))
 
         def deal(copy, dealt, raw, m_raw, m_lo, m_hi, t_lo=0, t_hi=PACK):
             copy(
@@ -96,91 +105,105 @@ def tile_picked_hmixharmelg_none_p_kernel(tc, x_words, x_scales, w1, gn, w2, w3,
         w2_raw = keep.tile([P, PACK, N], F32, name="w2_raw", tag="w1_then_w2")
         nc.sync.dma_start(w2_raw[:], w2.rearrange("(p j) c -> p j c", j=PACK))
 
+        w1_mx = [mx_tiles("w1_%d" % t, P) for t in range(PACK)]
         y_ps = [psum.tile([P, S], F32, name="y_ps%d" % t) for t in range(PACK)]
-        y_win = [keep.tile([P, S], F32, name="y_win%d" % t) for t in range(PACK)]
         for t in range(PACK):
-            words, plane = mx_tiles("w1_%d" % t, P)
+            words, plane = w1_mx[t]
             nc.vector.quantize_mx(words[:].bitcast(FP8X4), plane[:], w1_bf[:, t].rearrange("p m j -> p (m j)"))
             nc.tensor.matmul_mx(
                 y_ps[t][:], lhsT=words[:].bitcast(FP8X4), lhsT_scale=plane[:],
                 rhs=xq_words[:].bitcast(FP8X4), rhs_scale=x_plane[:, :S], start=True, stop=True,
             )
         for t in range(PACK):
-            nc.vector.tensor_copy(y_win[t][:], y_ps[t][:])
+            nc.vector.tensor_copy(y_win[t][:, :S], y_ps[t][:])
 
         def halves(name):
-            return [keep.tile([P, PACK, HALF], F32, name="%s%d" % (name, half)) for half in range(2)]
+            return [keep.tile([P, PACK, HALF], F32, name="%s%d" % (name, half), tag="%s%d" % (name, half), align_bytes=64) for half in range(2)]
 
-        pa, pa_sq, num, sq_sum, root, inv = (halves(name) for name in ("pa", "pa_sq", "num", "sq_sum", "root", "inv"))
-        y_sq = keep.tile([P, 2, PACK, HALF], F32, name="y_sq")
+        pa_sq, sq_sum, root, inv = (halves(name) for name in ("pa_sq", "sq_sum", "root", "inv"))
+        y_sq = keep.tile([P, PACK, S], F32, name="y_sq")
+        pa = keep.tile([P, PACK, S], F32, name="pa")
+        num = keep.tile([P, PACK, S], F32, name="num")
         z_words, z_plane = mx_tiles("z", S)
 
-        def fetch(half):
+        def fetch():
             for t in range(PACK):
-                nc.scalar.activation(pa[half][:, t, :], y_win[t][:].indirect(n1_sb[:, 8 * half : 8 * (half + 1)]), ACT.Copy)
+                nc.scalar.activation(pa[:, t, :], y_win[t][:].indirect(n1_sb[:]), ACT.Copy)
 
-        def numerator(half):
-            for t in range(PACK):
-                nc.vector.scalar_tensor_tensor(
-                    num[half][:, t, :], pa[half][:, t, :], gn_sb[:, t : t + 1],
-                    y_ps[t][:, HALF * half : HALF * (half + 1)], ALU.mult, ALU.mult,
-                )
+        def numerator(tiles):
+            for t in tiles:
+                nc.vector.scalar_tensor_tensor(num[:, t, :], pa[:, t, :], gn_sb[:, t : t + 1], y_ps[t][:], ALU.mult, ALU.mult)
 
         def square_sum(half):
-            nc.scalar.activation(pa_sq[half][:], pa[half][:], ACT.Square)
-            nc.vector.tensor_tensor(sq_sum[half][:], pa_sq[half][:], y_sq[:, half], ALU.add)
+            cols = slice(HALF * half, HALF * (half + 1))
+            nc.scalar.activation(pa_sq[half][:], pa[:, :, cols], ACT.Square)
+            nc.vector.tensor_tensor(sq_sum[half][:], pa_sq[half][:], y_sq[:, :, cols], ALU.add)
 
         def inverse(half):
             nc.scalar.activation(root[half][:], sq_sum[half][:], ACT.Abs_reciprocal_sqrt, bias=0.25, scale=0.5)
             nc.scalar.activation(inv[half][:], root[half][:], ACT.Square)
 
         def make_z(half):
-            z_bf = keep.tile([P, HALF, PACK], BF16, name="z_bf%d" % half, align_bytes=64)
+            z_bf = keep.tile([P, HALF, PACK], BF16, name="z_bf%d" % half, tag="z_bf%d" % half, align_bytes=64)
+            cols = slice(HALF * half, HALF * (half + 1))
             nc.vector.tensor_tensor(
                 z_bf[:].rearrange("p (c i) t -> p c t i", i=4),
-                num[half][:].rearrange("p t (c i) -> p c t i", i=4),
+                num[:, :, cols].rearrange("p t (c i) -> p c t i", i=4),
                 inv[half][:].rearrange("p t (c i) -> p c t i", i=4),
                 ALU.mult,
             )
-            cols = slice(HALF * half, HALF * (half + 1))
             nc.vector.quantize_mx(z_words[:, cols].bitcast(FP8X4), z_plane[:, cols], z_bf[:].rearrange("p c t -> p (c t)"))
 
-        w3_bf = keep.tile([P, PACK, P, PACK], BF16, name="w3_bf", align_bytes=64)
-        w3_words, w3_plane = mx_tiles("w3", N)
-        w2_mx = [mx_tiles("w2_%d" % pair, N // 2) for pair in range(2)]
-        w2_bf = [keep.tile([P, 2, P, PACK], BF16, name="w2_bf%d" % pair, align_bytes=64) for pair in range(2)]
+        def round_pair(copy, raw, pair, name, tag):
+            dealt = keep.tile([P, 2, P, PACK], BF16, name=name, tag=tag, align_bytes=64)
+            deal(copy, dealt, raw[:], 0, 0, P, 2 * pair, 2 * pair + 2)
+            return dealt
 
-        def round_w2(pair):
-            deal(nc.vector.tensor_copy, w2_bf[pair], w2_raw[:], 0, 0, P, 2 * pair, 2 * pair + 2)
-
-        def quantize_w2(pair):
-            words, plane = w2_mx[pair]
-            nc.vector.quantize_mx(words[:].bitcast(FP8X4), plane[:], w2_bf[pair][:].rearrange("p t m j -> p (t m j)"))
-
-        fetch(0)
-        for t in range(PACK):
-            nc.scalar.activation(y_sq[:, :, t, :], y_win[t][:].rearrange("p (u c) -> p u c", u=2), ACT.Square)
-        deal(nc.vector.tensor_copy, w3_bf, w3_raw[:], 0, 0, P)
-        numerator(0)
-        square_sum(0)
-        fetch(1)
-        nc.vector.quantize_mx(w3_words[:].bitcast(FP8X4), w3_plane[:], w3_bf[:].rearrange("p t m j -> p (t m j)"))
-        inverse(0)
-        round_w2(0)
-        square_sum(1)
-        numerator(1)
-        inverse(1)
-        quantize_w2(0)
-        make_z(0)
-        make_z(1)
+        def quantize_pair(dealt, name):
+            words, plane = mx_tiles(name, 2 * P)
+            nc.vector.quantize_mx(words[:].bitcast(FP8X4), plane[:], dealt[:].rearrange("p t m j -> p (t m j)"))
+            return words, plane
 
         h_ps = [psum.tile([P, S], F32, name="h_ps%d" % t) for t in range(PACK)]
-        for t in range(PACK):
-            cols = slice(P * t, P * (t + 1))
+
+        def add_product(t, weight, words, plane, cols, start, stop):
+            rows = slice(P * (t % 2), P * (t % 2 + 1))
             nc.tensor.matmul_mx(
-                h_ps[t][:], lhsT=w3_words[:, cols].bitcast(FP8X4), lhsT_scale=w3_plane[:, cols],
-                rhs=xtwo_words[:].bitcast(FP8X4), rhs_scale=x_plane[:, S:], start=True, stop=False,
+                h_ps[t][:, cols], lhsT=weight[0][:, rows].bitcast(FP8X4), lhsT_scale=weight[1][:, rows],
+                rhs=words.bitcast(FP8X4), rhs_scale=plane, start=start, stop=stop,
             )
+
+        def w3_product(t, weight):
+            add_product(t, weight, xtwo_words[:], x_plane[:, S:], slice(0, S), True, False)
+
+        def w2_product(t, weight, half):
+            cols = slice(HALF * half, HALF * (half + 1))
+            add_product(t, weight, z_words[:, cols], z_plane[:, cols], cols, False, half == 1)
+
+        fetch()
+        for t in range(2):
+            nc.scalar.activation(y_sq[:, t, :], y_win[t][:, :S], ACT.Square)
+        for t in range(2, PACK):
+            nc.vector.tensor_tensor(y_sq[:, t, :], y_ps[t][:], y_win[t][:, :S], ALU.mult)
+        w3_bf = round_pair(nc.vector.tensor_copy, w3_raw, 0, "w3_bf_lo", "w3_bf_lo")
+        numerator(range(PACK - 1))
+        square_sum(0)
+        square_sum(1)
+        numerator([PACK - 1])
+        inverse(0)
+        w2_bf = round_pair(nc.vector.tensor_copy, w2_raw, 0, "w2_bf_lo", "w2_bf_lo")
+        w3_mx = quantize_pair(w3_bf, "w3_lo")
+        inverse(1)
+        w2_mx = quantize_pair(w2_bf, "w2_lo")
+        make_z(0)
+        make_z(1)
+        for t in range(2):
+            w3_product(t, w3_mx)
+        for half in range(2):
+            for t in range(2):
+                w2_product(t, w2_mx, half)
+        w3_bf = round_pair(nc.scalar.copy, w3_raw, 1, "w3_bf_hi", "root1")
+        w2_bf = round_pair(nc.vector.tensor_copy, w2_raw, 1, "w2_bf_hi", "z_bf1")
 
         top = keep.tile([P, PACK], F32, name="top")
         shift = keep.tile([P, PACK], F32, name="shift", tag="shift_then_log")
@@ -189,14 +212,11 @@ def tile_picked_hmixharmelg_none_p_kernel(tc, x_words, x_scales, w1, gn, w2, w3,
         ea_sum = keep.tile([P, PACK, S], F32, name="ea_sum")
         for t in range(PACK):
             if t == 2:
-                round_w2(1)
-                quantize_w2(1)
-            words, plane = w2_mx[t // 2]
-            cols = slice(P * (t % 2), P * (t % 2 + 1))
-            nc.tensor.matmul_mx(
-                h_ps[t][:], lhsT=words[:, cols].bitcast(FP8X4), lhsT_scale=plane[:, cols],
-                rhs=z_words[:].bitcast(FP8X4), rhs_scale=z_plane[:], start=False, stop=True,
-            )
+                w3_mx = quantize_pair(w3_bf, "w3_hi")
+                w2_mx = quantize_pair(w2_bf, "w2_hi")
+                for u in range(2, PACK):
+                    w3_product(u, w3_mx)
+                    add_product(u, w2_mx, z_words[:], z_plane[:], slice(0, S), False, True)
             col = slice(t, t + 1)
             nc.vector.tensor_scalar(h_win[t][:, :S], h_ps[t][:], 1.0, None, ALU.mult, ALU.max, accum_out=top[:, col])
             nc.vector.tensor_scalar(shift[:, col], top[:, col], tau_sb[:, col], -1.0, ALU.mult, ALU.mult)

@@ -18,8 +18,6 @@ ALU = mybir.AluOpType
 P = 128
 PACK = 4
 HALF = S // 2
-M_SPLIT = 104
-X_SPLIT = 512
 
 
 def tile_picked_hmixharmelg_none_p_kernel(tc, x_words, x_scales, w1, gn, w2, w3, tau, offs, n1, two, n2, n3, out):
@@ -36,21 +34,20 @@ def tile_picked_hmixharmelg_none_p_kernel(tc, x_words, x_scales, w1, gn, w2, w3,
         scale_table = keep.tile([P, T], U8, name="scale_table", tag="scales_then_w3", align_bytes=64)
         nc.vector.memset(scale_table[:, : T // 2].bitcast(I32), 0)
         nc.gpsimd.memset(scale_table[:, T // 2 :].bitcast(I32), 0)
-        word_table = keep.tile([P, T], I32, name="word_table", tag="words_then_gn", align_bytes=64)
-        word_rows = x_words[0].rearrange("p n t -> p (n t)").bitcast(I32)
-        nc.sync.dma_start(word_table[:, :X_SPLIT], word_rows[:, :X_SPLIT])
+        w1_raw = keep.tile([P, PACK * H], F32, name="w1_raw", tag="w1_then_w2")
+        w1_rows = w1.rearrange("(p j) c -> p (j c)", j=PACK)
+        nc.sync.dma_start(w1_raw[:, :H], w1_rows[:, :H])
         offs_sb = load_list(offs, "offs_sb")
         two_sb = load_list(two, "two_sb")
         n1_sb = load_list(n1, "n1_sb")
         scale_rows = x_scales[0].bitcast(I32)
         for b in range(2):
             nc.sync.dma_start(scale_table[:].bitcast(I32)[b:P:16, :], scale_rows[b:16:2, :])
-        nc.sync.dma_start(word_table[:, X_SPLIT:], word_rows[:, X_SPLIT:])
-
-        w1_halves = keep.tile([P, 2, PACK, H // 2], F32, name="w1_halves", tag="w1_then_w2")
-        w1_raw = [w1_halves[:, half] for half in range(2)]
-        for half in range(2):
-            nc.sync.dma_start(w1_raw[half], w1.rearrange("(p j) c -> p j c", j=PACK)[:, :, 256 * half : 256 * (half + 1)])
+        nc.sync.dma_start(w1_raw[:, H:], w1_rows[:, H:])
+        word_table = keep.tile([P, T], I32, name="word_table", align_bytes=64)
+        nc.sync.dma_start(word_table[:], x_words[0].rearrange("p n t -> p (n t)").bitcast(I32))
+        gn_sb = keep.tile([P, PACK], F32, name="gn_sb")
+        nc.sync.dma_start(gn_sb[:], gn.rearrange("(p t) o -> p (t o)", t=PACK))
         n2_sb = load_list(n2, "n2_sb")
         n3_sb = load_list(n3, "n3_sb")
 
@@ -82,36 +79,32 @@ def tile_picked_hmixharmelg_none_p_kernel(tc, x_words, x_scales, w1, gn, w2, w3,
         nc.vector.tensor_copy(xq_words[:], word_table[:].bitcast(U32).indirect(offs_sb[:]))
         xtwo_words = keep.tile([P, S], U32, name="xtwo_words", align_bytes=64)
         nc.vector.tensor_copy(xtwo_words[:], word_table[:].bitcast(U32).indirect(two_sb[:]))
-        gn_sb = keep.tile([P, PACK], F32, name="gn_sb", tag="words_then_gn", align_bytes=64)
-        nc.sync.dma_start(gn_sb[:], gn.rearrange("(p t) o -> p (t o)", t=PACK))
         tau_sb = keep.tile([P, PACK], F32, name="tau_sb", tag="bytes_then_tau", align_bytes=64)
         nc.sync.dma_start(tau_sb[:], tau.rearrange("(p t) o -> p (t o)", t=PACK))
 
-        def deal(copy, dealt, raw, m_raw, m_lo, m_hi, t_lo=0, t_hi=PACK):
+        def deal(copy, dealt, raw, t_lo, t_hi):
             copy(
-                dealt[:, :, m_lo:m_hi, :].rearrange("p t m j -> p m j t"),
-                raw.rearrange("p j (m t) -> p m j t", t=PACK)[:, m_lo - m_raw : m_hi - m_raw, :, t_lo:t_hi],
+                dealt[:].rearrange("p t m j -> p m j t"),
+                raw.rearrange("p j (m t) -> p m j t", t=PACK)[:, :, :, t_lo:t_hi],
             )
 
-        def mx_tiles(name, width):
-            words = keep.tile([P, width], U32, name=name + "_words", align_bytes=64)
+        def mx_tiles(name, width, tag=""):
+            words = keep.tile([P, width], U32, name=name + "_words", tag=tag, align_bytes=64)
             plane = keep.tile([P, width], U8, name=name + "_plane", align_bytes=64)
             return words, plane
 
         w1_bf = keep.tile([P, PACK, P, PACK], BF16, name="w1_bf", align_bytes=64)
-        deal(nc.vector.tensor_copy, w1_bf, w1_raw[0], 0, 0, 64)
-        deal(nc.vector.tensor_copy, w1_bf, w1_raw[1], 64, 64, M_SPLIT)
-        deal(nc.scalar.copy, w1_bf, w1_raw[1], 64, M_SPLIT, P)
+        deal(nc.vector.tensor_copy, w1_bf, w1_raw[:].rearrange("p (j c) -> p j c", j=PACK), 0, PACK)
         w2_raw = keep.tile([P, PACK, N], F32, name="w2_raw", tag="w1_then_w2")
         nc.sync.dma_start(w2_raw[:], w2.rearrange("(p j) c -> p j c", j=PACK))
 
-        w1_mx = [mx_tiles("w1_%d" % t, P) for t in range(PACK)]
+        w1_words, w1_plane = mx_tiles("w1", H)
+        nc.vector.quantize_mx(w1_words[:].bitcast(FP8X4), w1_plane[:], w1_bf[:].rearrange("p t m j -> p (t m j)"))
         y_ps = [psum.tile([P, S], F32, name="y_ps%d" % t) for t in range(PACK)]
         for t in range(PACK):
-            words, plane = w1_mx[t]
-            nc.vector.quantize_mx(words[:].bitcast(FP8X4), plane[:], w1_bf[:, t].rearrange("p m j -> p (m j)"))
+            rows = slice(P * t, P * (t + 1))
             nc.tensor.matmul_mx(
-                y_ps[t][:], lhsT=words[:].bitcast(FP8X4), lhsT_scale=plane[:],
+                y_ps[t][:], lhsT=w1_words[:, rows].bitcast(FP8X4), lhsT_scale=w1_plane[:, rows],
                 rhs=xq_words[:].bitcast(FP8X4), rhs_scale=x_plane[:, :S], start=True, stop=True,
             )
         for t in range(PACK):
@@ -121,7 +114,7 @@ def tile_picked_hmixharmelg_none_p_kernel(tc, x_words, x_scales, w1, gn, w2, w3,
             return [keep.tile([P, PACK, HALF], F32, name="%s%d" % (name, half), tag="%s%d" % (name, half), align_bytes=64) for half in range(2)]
 
         pa_sq, sq_sum, root, inv = (halves(name) for name in ("pa_sq", "sq_sum", "root", "inv"))
-        y_sq = keep.tile([P, PACK, S], F32, name="y_sq")
+        y_sq = keep.tile([P, PACK, S], F32, name="y_sq", tag="y_sq", align_bytes=64)
         pa = keep.tile([P, PACK, S], F32, name="pa")
         num = keep.tile([P, PACK, S], F32, name="num")
         z_words, z_plane = mx_tiles("z", S)
@@ -156,11 +149,11 @@ def tile_picked_hmixharmelg_none_p_kernel(tc, x_words, x_scales, w1, gn, w2, w3,
 
         def round_pair(copy, raw, pair, name, tag):
             dealt = keep.tile([P, 2, P, PACK], BF16, name=name, tag=tag, align_bytes=64)
-            deal(copy, dealt, raw[:], 0, 0, P, 2 * pair, 2 * pair + 2)
+            deal(copy, dealt, raw[:], 2 * pair, 2 * pair + 2)
             return dealt
 
-        def quantize_pair(dealt, name):
-            words, plane = mx_tiles(name, 2 * P)
+        def quantize_pair(dealt, name, tag=""):
+            words, plane = mx_tiles(name, 2 * P, tag)
             nc.vector.quantize_mx(words[:].bitcast(FP8X4), plane[:], dealt[:].rearrange("p t m j -> p (t m j)"))
             return words, plane
 
@@ -173,36 +166,38 @@ def tile_picked_hmixharmelg_none_p_kernel(tc, x_words, x_scales, w1, gn, w2, w3,
                 rhs=words.bitcast(FP8X4), rhs_scale=plane, start=start, stop=stop,
             )
 
-        def w3_product(t, weight):
-            add_product(t, weight, xtwo_words[:], x_plane[:, S:], slice(0, S), True, False)
-
         def w2_product(t, weight, half):
             cols = slice(HALF * half, HALF * (half + 1))
             add_product(t, weight, z_words[:, cols], z_plane[:, cols], cols, False, half == 1)
 
         fetch()
-        for t in range(2):
+        for t in range(PACK - 1):
             nc.scalar.activation(y_sq[:, t, :], y_win[t][:, :S], ACT.Square)
-        for t in range(2, PACK):
+        for t in range(PACK - 1, PACK):
             nc.vector.tensor_tensor(y_sq[:, t, :], y_ps[t][:], y_win[t][:, :S], ALU.mult)
-        w3_bf = round_pair(nc.vector.tensor_copy, w3_raw, 0, "w3_bf_lo", "w3_bf_lo")
+        w3_bf = keep.tile([P, PACK, P, PACK], BF16, name="w3_bf", align_bytes=64)
+        deal(nc.vector.tensor_copy, w3_bf, w3_raw[:], 0, PACK)
         numerator(range(PACK - 1))
         square_sum(0)
         square_sum(1)
         numerator([PACK - 1])
         inverse(0)
-        w2_bf = round_pair(nc.vector.tensor_copy, w2_raw, 0, "w2_bf_lo", "w2_bf_lo")
-        w3_mx = quantize_pair(w3_bf, "w3_lo")
+        w2_bf = round_pair(nc.vector.tensor_copy, w2_raw, 0, "w2_bf_lo", "pa_sq1")
+        w3_words, w3_plane = mx_tiles("w3", N, "y_sq")
+        nc.vector.quantize_mx(w3_words[:].bitcast(FP8X4), w3_plane[:], w3_bf[:].rearrange("p t m j -> p (t m j)"))
         inverse(1)
         w2_mx = quantize_pair(w2_bf, "w2_lo")
         make_z(0)
         make_z(1)
-        for t in range(2):
-            w3_product(t, w3_mx)
+        for t in range(PACK):
+            rows = slice(P * t, P * (t + 1))
+            nc.tensor.matmul_mx(
+                h_ps[t][:], lhsT=w3_words[:, rows].bitcast(FP8X4), lhsT_scale=w3_plane[:, rows],
+                rhs=xtwo_words[:].bitcast(FP8X4), rhs_scale=x_plane[:, S:], start=True, stop=False,
+            )
         for half in range(2):
             for t in range(2):
                 w2_product(t, w2_mx, half)
-        w3_bf = round_pair(nc.scalar.copy, w3_raw, 1, "w3_bf_hi", "root1")
         w2_bf = round_pair(nc.vector.tensor_copy, w2_raw, 1, "w2_bf_hi", "z_bf1")
 
         top = keep.tile([P, PACK], F32, name="top")
@@ -212,10 +207,8 @@ def tile_picked_hmixharmelg_none_p_kernel(tc, x_words, x_scales, w1, gn, w2, w3,
         ea_sum = keep.tile([P, PACK, S], F32, name="ea_sum")
         for t in range(PACK):
             if t == 2:
-                w3_mx = quantize_pair(w3_bf, "w3_hi")
                 w2_mx = quantize_pair(w2_bf, "w2_hi")
                 for u in range(2, PACK):
-                    w3_product(u, w3_mx)
                     add_product(u, w2_mx, z_words[:], z_plane[:], slice(0, S), False, True)
             col = slice(t, t + 1)
             nc.vector.tensor_scalar(h_win[t][:, :S], h_ps[t][:], 1.0, None, ALU.mult, ALU.max, accum_out=top[:, col])

from contextlib import ExitStack

import concourse.mybir as mybir

K, T, S, N, H = 512, 2048, 256, 512, 512
FLOPS = 2 * S * (K * H + H * N + K * N)

F32 = mybir.dt.float32
BF16 = mybir.dt.bfloat16
I32 = mybir.dt.int32
U32 = mybir.dt.uint32
U16 = mybir.dt.uint16
U8 = mybir.dt.uint8
FP8X4 = mybir.dt.float8_e4m3fn_x4
ACT = mybir.ActivationFunctionType
ALU = mybir.AluOpType

P = 128
PACK = 4
HALF = S // 2


def tile_picked_hmixharmelg_none_p_kernel(tc, x_words, x_scales, w1, gn, w2, w3, tau, offs, n1, two, n2, n3, out):
    nc = tc.nc
    with ExitStack() as ctx:
        keep = ctx.enter_context(tc.tile_pool(name="keep", bufs=1))
        psum = ctx.enter_context(tc.psum_pool(name="psum", bufs=1))

        def load_list(src, name):
            tile = keep.tile([P, S // 16], U16, name=name)
            nc.sync.dma_start(tile[:], src)
            return tile

        scale_table = keep.tile([P, T], U8, name="scale_table", tag="scales_then_w3", align_bytes=64)
        nc.vector.memset(scale_table[:, : T // 2].bitcast(I32), 0)
        nc.gpsimd.memset(scale_table[:, T // 2 :].bitcast(I32), 0)
        w1_raw = keep.tile([P, PACK * H], F32, name="w1_raw", tag="w1_then_w2")
        w1_rows = w1.rearrange("(p j) c -> p (j c)", j=PACK)
        nc.sync.dma_start(w1_raw[:, :H], w1_rows[:, :H])
        offs_sb = load_list(offs, "offs_sb")
        two_sb = load_list(two, "two_sb")
        n1_sb = load_list(n1, "n1_sb")
        scale_rows = x_scales[0].bitcast(I32)
        for b in range(2):
            nc.sync.dma_start(scale_table[:].bitcast(I32)[b:P:16, :], scale_rows[b:16:2, :])
        nc.sync.dma_start(w1_raw[:, H:], w1_rows[:, H:])
        word_table = keep.tile([P, T], I32, name="word_table", align_bytes=64)
        nc.sync.dma_start(word_table[:], x_words[0].rearrange("p n t -> p (n t)").bitcast(I32))
        gn_sb = keep.tile([P, PACK], F32, name="gn_sb")
        nc.sync.dma_start(gn_sb[:], gn.rearrange("(p t) o -> p (t o)", t=PACK))
        n2_sb = load_list(n2, "n2_sb")
        n3_sb = load_list(n3, "n3_sb")

        warm_in = keep.tile([P, 1], F32, name="warm_in")
        warm_out = keep.tile([P, 1], F32, name="warm_out")
        nc.gpsimd.memset(warm_in[:], 1.0)
        nc.scalar.activation(warm_out[:], warm_in[:], ACT.Abs_reciprocal_sqrt, bias=0.25, scale=0.5)

        h_win = [keep.tile([P, 2 * S], F32, name="h_win%d" % t) for t in range(PACK)]
        y_win = [keep.tile([P, S + 16], F32, name="y_win%d" % t) for t in range(PACK)]
        for t in range(PACK):
            nc.vector.memset(y_win[t][:, S:], 0.0)
            nc.vector.memset(h_win[t][:, S:], 0.0)

        x_plane = keep.tile([P, 2 * S], U8, name="x_plane", align_bytes=64)
        nc.vector.memset(x_plane[:].bitcast(I32), 0)
        picked_bytes = keep.tile([P, 2 * S], U8, name="picked_bytes", tag="bytes_then_tau", align_bytes=64)
        nc.vector.tensor_copy(picked_bytes[:, :S], scale_table[:].indirect(offs_sb[:]))
        nc.vector.tensor_copy(picked_bytes[:, S:], scale_table[:].indirect(two_sb[:]))
        for q in range(4):
            rows = slice(32 * q, 32 * q + 2)
            nc.vector.tensor_copy(x_plane[:].bitcast(I32)[rows, :], picked_bytes[:].bitcast(I32)[rows, :])
        for b in range(2):
            nc.sync.dma_start(x_plane[:].bitcast(I32)[2 + b : P : 32, :], picked_bytes[:].bitcast(I32)[16 + b : P : 32, :])
        w3_raw = keep.tile([P, PACK, N], F32, name="w3_raw", tag="scales_then_w3", align_bytes=64)
        nc.sync.dma_start(w3_raw[:], w3.rearrange("(p j) c -> p j c", j=PACK))

        xq_words = keep.tile([P, S], U32, name="xq_words", align_bytes=64)
        nc.vector.tensor_copy(xq_words[:], word_table[:].bitcast(U32).indirect(offs_sb[:]))
        xtwo_words = keep.tile([P, S], U32, name="xtwo_words", align_bytes=64)
        nc.vector.tensor_copy(xtwo_words[:], word_table[:].bitcast(U32).indirect(two_sb[:]))
        tau_sb = keep.tile([P, PACK], F32, name="tau_sb", tag="bytes_then_tau", align_bytes=64)
        nc.sync.dma_start(tau_sb[:], tau.rearrange("(p t) o -> p (t o)", t=PACK))

        def deal(copy, dealt, raw, t_lo, t_hi):
            copy(
                dealt[:].rearrange("p t m j -> p m j t"),
                raw.rearrange("p j (m t) -> p m j t", t=PACK)[:, :, :, t_lo:t_hi],
            )

        def mx_tiles(name, width, tag=""):
            words = keep.tile([P, width], U32, name=name + "_words", tag=tag, align_bytes=64)
            plane = keep.tile([P, width], U8, name=name + "_plane", align_bytes=64)
            return words, plane

        w1_bf = keep.tile([P, PACK, P, PACK], BF16, name="w1_bf", align_bytes=64)
        deal(nc.vector.tensor_copy, w1_bf, w1_raw[:].rearrange("p (j c) -> p j c", j=PACK), 0, PACK)
        w2_raw = keep.tile([P, PACK, N], F32, name="w2_raw", tag="w1_then_w2")
        nc.sync.dma_start(w2_raw[:], w2.rearrange("(p j) c -> p j c", j=PACK))

        w1_words, w1_plane = mx_tiles("w1", H)
        nc.vector.quantize_mx(w1_words[:].bitcast(FP8X4), w1_plane[:], w1_bf[:].rearrange("p t m j -> p (t m j)"))
        y_ps = [psum.tile([P, S], F32, name="y_ps%d" % t) for t in range(PACK)]
        for t in range(PACK):
            rows = slice(P * t, P * (t + 1))
            nc.tensor.matmul_mx(
                y_ps[t][:], lhsT=w1_words[:, rows].bitcast(FP8X4), lhsT_scale=w1_plane[:, rows],
                rhs=xq_words[:].bitcast(FP8X4), rhs_scale=x_plane[:, :S], start=True, stop=True,
            )
        for t in range(PACK):
            nc.vector.tensor_copy(y_win[t][:, :S], y_ps[t][:])

        def halves(name):
            return [keep.tile([P, PACK, HALF], F32, name="%s%d" % (name, half), tag="%s%d" % (name, half), align_bytes=64) for half in range(2)]

        pa_sq, sq_sum, root, inv = (halves(name) for name in ("pa_sq", "sq_sum", "root", "inv"))
        y_sq = keep.tile([P, PACK, S], F32, name="y_sq", tag="y_sq", align_bytes=64)
        pa = keep.tile([P, PACK, S], F32, name="pa")
        num = keep.tile([P, PACK, S], F32, name="num")
        z_words, z_plane = mx_tiles("z", S)

        def fetch():
            for t in range(PACK):
                nc.scalar.activation(pa[:, t, :], y_win[t][:].indirect(n1_sb[:]), ACT.Copy)

        def numerator(tiles):
            for t in tiles:
                nc.vector.scalar_tensor_tensor(num[:, t, :], pa[:, t, :], gn_sb[:, t : t + 1], y_ps[t][:], ALU.mult, ALU.mult)

        def square_sum(half):
            cols = slice(HALF * half, HALF * (half + 1))
            nc.scalar.activation(pa_sq[half][:], pa[:, :, cols], ACT.Square)
            nc.vector.tensor_tensor(sq_sum[half][:], pa_sq[half][:], y_sq[:, :, cols], ALU.add)

        def inverse(half):
            nc.scalar.activation(root[half][:], sq_sum[half][:], ACT.Abs_reciprocal_sqrt, bias=0.25, scale=0.5)
            nc.scalar.activation(inv[half][:], root[half][:], ACT.Square)

        def make_z(half):
            z_bf = keep.tile([P, HALF, PACK], BF16, name="z_bf%d" % half, tag="z_bf%d" % half, align_bytes=64)
            cols = slice(HALF * half, HALF * (half + 1))
            nc.vector.tensor_tensor(
                z_bf[:].rearrange("p (c i) t -> p c t i", i=4),
                num[:, :, cols].rearrange("p t (c i) -> p c t i", i=4),
                inv[half][:].rearrange("p t (c i) -> p c t i", i=4),
                ALU.mult,
            )
            nc.vector.quantize_mx(z_words[:, cols].bitcast(FP8X4), z_plane[:, cols], z_bf[:].rearrange("p c t -> p (c t)"))

        def round_pair(copy, raw, pair, name, tag):
            dealt = keep.tile([P, 2, P, PACK], BF16, name=name, tag=tag, align_bytes=64)
            deal(copy, dealt, raw[:], 2 * pair, 2 * pair + 2)
            return dealt

        def quantize_pair(dealt, name, tag=""):
            words, plane = mx_tiles(name, 2 * P, tag)
            nc.vector.quantize_mx(words[:].bitcast(FP8X4), plane[:], dealt[:].rearrange("p t m j -> p (t m j)"))
            return words, plane

        h_ps = [psum.tile([P, S], F32, name="h_ps%d" % t) for t in range(PACK)]

        def add_product(t, weight, words, plane, cols, start, stop):
            rows = slice(P * (t % 2), P * (t % 2 + 1))
            nc.tensor.matmul_mx(
                h_ps[t][:, cols], lhsT=weight[0][:, rows].bitcast(FP8X4), lhsT_scale=weight[1][:, rows],
                rhs=words.bitcast(FP8X4), rhs_scale=plane, start=start, stop=stop,
            )

        def w2_product(t, weight, half):
            cols = slice(HALF * half, HALF * (half + 1))
            add_product(t, weight, z_words[:, cols], z_plane[:, cols], cols, False, half == 1)

        fetch()
        for t in range(PACK - 1):
            nc.scalar.activation(y_sq[:, t, :], y_win[t][:, :S], ACT.Square)
        for t in range(PACK - 1, PACK):
            nc.vector.tensor_tensor(y_sq[:, t, :], y_ps[t][:], y_win[t][:, :S], ALU.mult)
        w3_bf = keep.tile([P, PACK, P, PACK], BF16, name="w3_bf", align_bytes=64)
        deal(nc.vector.tensor_copy, w3_bf, w3_raw[:], 0, PACK)
        numerator(range(PACK - 1))
        square_sum(0)
        square_sum(1)
        numerator([PACK - 1])
        inverse(0)
        w2_bf = round_pair(nc.vector.tensor_copy, w2_raw, 0, "w2_bf_lo", "pa_sq1")
        w3_words, w3_plane = mx_tiles("w3", N, "y_sq")
        nc.vector.quantize_mx(w3_words[:].bitcast(FP8X4), w3_plane[:], w3_bf[:].rearrange("p t m j -> p (t m j)"))
        inverse(1)
        w2_mx = quantize_pair(w2_bf, "w2_lo")
        make_z(0)
        make_z(1)
        for t in range(PACK):
            rows = slice(P * t, P * (t + 1))
            nc.tensor.matmul_mx(
                h_ps[t][:], lhsT=w3_words[:, rows].bitcast(FP8X4), lhsT_scale=w3_plane[:, rows],
                rhs=xtwo_words[:].bitcast(FP8X4), rhs_scale=x_plane[:, S:], start=True, stop=False,
            )
        for half in range(2):
            for t in range(2):
                w2_product(t, w2_mx, half)
        w2_bf = round_pair(nc.vector.tensor_copy, w2_raw, 1, "w2_bf_hi", "z_bf1")

        top = keep.tile([P, PACK], F32, name="top")
        shift = keep.tile([P, PACK], F32, name="shift", tag="shift_then_log")
        ea = keep.tile([P, PACK, S], F32, name="ea")
        ea2 = keep.tile([P, PACK, S], F32, name="ea2")
        ea_sum = keep.tile([P, PACK, S], F32, name="ea_sum")
        for t in range(PACK):
            if t == 2:
                w2_mx = quantize_pair(w2_bf, "w2_hi")
                for u in range(2, PACK):
                    add_product(u, w2_mx, z_words[:], z_plane[:], slice(0, S), False, True)
            col = slice(t, t + 1)
            nc.vector.tensor_scalar(h_win[t][:, :S], h_ps[t][:], 1.0, None, ALU.mult, ALU.max, accum_out=top[:, col])
            nc.vector.tensor_scalar(shift[:, col], top[:, col], tau_sb[:, col], -1.0, ALU.mult, ALU.mult)
            nc.scalar.activation(ea[:, t, :], h_win[t][:].indirect(n2_sb[:]), ACT.Exp, bias=shift[:, col], scale=tau_sb[:, col])
            nc.scalar.activation(ea2[:, t, :], h_win[t][:].indirect(n3_sb[:]), ACT.Exp, bias=shift[:, col], scale=tau_sb[:, col])
        for t in range(PACK):
            nc.vector.tensor_tensor(ea_sum[:, t, :], ea[:, t, :], ea2[:, t, :], ALU.add)

        logs = keep.tile([P, PACK, S], F32, name="logs", tag="shift_then_log")
        res = keep.tile([P, PACK, S], F32, name="res")
        out_rows = out.rearrange("(p t) j -> p t j", t=PACK)
        for t in range(PACK):
            nc.scalar.activation(logs[:, t, :], ea_sum[:, t, :], ACT.Ln, bias=0.25)
            nc.vector.tensor_tensor(res[:, t, :], h_ps[t][:], logs[:, t, :], ALU.add)
            nc.sync.dma_start(out_rows[:, t, :], res[:, t, :])
